import numpy as np
CORES = [52,68,84,180,196,212,308,324,340]
N = 9
B, TIMES = 32, 2
def setup_inputs(rng):
    return {"x": (rng.standard_normal((N, 128, B), dtype=np.float32) * (0.5 + np.abs(rng.standard_normal((1, 1, B), dtype=np.float32))) / np.float32(np.sqrt(128 * N))), "a": (rng.standard_normal((N, 128, N * 128), dtype=np.float32) / 8)}
def reference(x, a):
    X, A = x.astype(np.float64), a.astype(np.float64)
    h = X
    for _ in range(TIMES):
        h = np.stack([sum(A[r][:, 128 * j:128 * j + 128].T @ h[j] for j in range(N)) for r in range(N)])
        h = h / np.sqrt((h ** 2).sum(axis=(0, 1)))
        h = h + X
    return {"y": h.astype(np.float32)}

import math
from concourse.bass import DstId, RemoteDMATransfer
from concourse.mybir import AluOpType, AxisListType, ActivationFunctionType

N, B, P = 9, 32, 128
GT = 3
NP = N // GT

SCRATCH = {
    "at": ("sbuf", [P, N * P], "float32"),
    "h1": ("sbuf", [P, N * B], "float32"),
    "h2": ("sbuf", [P, N * B], "float32"),
    "sq": ("sbuf", [P, N * B], "float32"),
    "ones": ("sbuf", [P, P], "float32"),
    "idn": ("sbuf", [P, 2 * B], "float32"),
    "prod": ("sbuf", [P, 2 * B], "float32"),
    "wsb": ("sbuf", [P, B], "float32"),
    "land": ("sbuf", [P, 12], "float32"),
    "fin": ("sbuf", [P, 12], "float32"),
    "rr": ("sbuf", [P, B], "float32"),
    "r2": ("sbuf", [P, B], "float32"),
    "xq": ("sbuf", [P, B], "float32"),
    "t1": ("sbuf", [P, B], "float32"),
    "vp": ("sbuf", [P, B], "float32"),
    "e1": ("sbuf", [P, B], "float32"),
    "ee": ("sbuf", [P, B], "float32"),
    "es": ("sbuf", [P, B], "float32"),
    "s3": ("sbuf", [P, 4], "float32"),
    "rt": ("sbuf", [P, B], "float32"),
    "rs": ("sbuf", [P, B], "float32"),
    "y1": ("sbuf", [P, B], "float32"),
    "yo": ("sbuf", [P, B], "float32"),
    "ups": ("psum", [P, 512], "float32"),
    "wps": ("psum", [P, 512], "float32"),
    "sps": ("psum", [P, 512], "float32"),
    "qps": ("psum", [P, 512], "float32"),
    "fps": ("psum", [P, 512], "float32"),
}
SEMAPHORES = (["xl", "init", "idn", "u", "uc", "w", "wc", "pa", "pv", "pq", "col", "cin", "cfin", "ssum", "r", "r2",
               "xq", "t1", "vp", "e1", "ee", "s3", "es", "f", "rt", "rs", "y1", "y2", "st", "sent"]
              + ["al%d" % k for k in range(NP)]
              + ["xa%d" % j for j in range(N)] + ["ua%d" % j for j in range(N)] + ["sq%d" % j for j in range(N)])

_PLAN = {}


def _mask(topo, src, dsts):
    m = topo.mask(src, dsts[0])
    for d in dsts[1:]:
        m &= topo.mask(src, d)
    return m


def _bits(m):
    return bin(m).count("1")


def _plan(T, topo):
    if "p" in _PLAN:
        return _PLAN["p"]
    cores = [int(c) for c in T.cores]
    n = len(cores)
    world = range(4 * topo.CORES_PER_HOST)
    taken = set(cores)
    others = [[j for j in range(n) if j != i] for i in range(n)]
    hubs = [i for i in range(n) if all(topo.may_write(cores[i], cores[j]) for j in others[i])]
    relay, relayed, direct = [], [], []
    for i in range(n):
        me = cores[i]
        far = [j for j in others[i] if not topo.may_write(me, cores[j])]
        near_die = [c for c in world if c not in taken and topo.chip(c) == topo.chip(me) and topo.die(c) == topo.die(me)]
        if far:
            rack = topo.rack(topo.host(cores[far[0]]))
            cand = [c for c in near_die if topo.rack(topo.host(c)) == rack and topo.may_write(me, c)
                    and all(topo.may_write(c, cores[j]) for j in far)]
            tgt = far
        else:
            cand = [c for c in near_die if topo.host(c) == topo.host(me)]
            tgt = [j for j in others[i] if topo.host(cores[j]) == topo.host(me)]
        taken.add(cand[0])
        relay.append(cand[0])
        relayed.append(sorted(tgt, key=lambda j: (j - i) % len(tgt)))
        direct.append(sorted([j for j in others[i] if j not in tgt], key=lambda j: ((j - i) % len(hubs), j)))
    cnt_d = [_bits(_mask(topo, cores[i], [relay[i]] + [cores[j] for j in direct[i]])) for i in range(n)]
    cnt_r = [_bits(_mask(topo, relay[i], [cores[j] for j in relayed[i]])) for i in range(n)]
    order, late, cnt = [], [], []
    for q in range(n):
        key = {q: (-1, 0)}
        c = {}
        for j in others[q]:
            if q in relayed[j]:
                key[j] = (1, relayed[j].index(q))
                c[j] = cnt_r[j]
            else:
                key[j] = (0, direct[j].index(q))
                c[j] = cnt_d[j]
        order.append(sorted(range(n), key=lambda j: key[j]))
        late.append(sum(1 for j in others[q] if q in relayed[j]))
        cnt.append(c)
    partners = {h: [q for q in range(n) if q not in hubs and topo.chip(cores[q]) == topo.chip(cores[h])] for h in hubs}
    p = {"cores": cores, "hubs": hubs, "relay": relay, "relayed": relayed, "direct": direct, "order": order,
         "late": late, "cnt": cnt, "cnt_d": cnt_d, "partners": partners,
         "relay_of": {relay[i]: i for i in range(n)}}
    _PLAN["p"] = p
    return p


def _send(g, topo, me, dsts, src, dst_aps, rsem, lsem):
    m = _mask(topo, me, dsts)
    ids = []
    for d in dsts:
        rid, pid = topo.addr(d, me)
        ids.append(DstId(rid=rid, pnc=pid))
    g.remote_dma_fused([RemoteDMATransfer(dst_ids=ids, dma_engine_mask=m, remote_sem=rsem, srcs=[src], dsts=dst_aps,
                                          alu_op=0)], local_sem=lsem)
    return _bits(m)


def _sl(buf, j):
    return buf[:, B * j:B * (j + 1)]


def _relay_program(g, core, T, topo, pl):
    i = pl["relay_of"][core]
    S = T.sem
    dsts = [pl["cores"][j] for j in pl["relayed"][i]]
    left = 0
    for buf, name in ((T.h1, "xa%d"), (T.h2, "ua%d")):
        g.wait_ge(S[name % i], pl["cnt_d"][i])
        left += _send(g, topo, core, dsts, _sl(buf, i), [_sl(buf, i) for _ in dsts], S[name % i], S.sent)
    g.wait_ge(S.sent, left)


def rank_program(g, core, T, topo):
    pl = _plan(T, topo)
    if core in pl["relay_of"]:
        _relay_program(g, core, T, topo, pl)
        return
    q = T.rank_of(core)
    if q is None:
        return
    S = T.sem
    v, pe, act, sy = g.vector, g.tensor, g.scalar, g.sync
    Act, Alu = ActivationFunctionType, AluOpType
    cores, hubs, order, cnt = pl["cores"], pl["hubs"], pl["order"][q], pl["cnt"][q]
    is_hub = q in hubs
    x_own, u_own = _sl(T.h1, q), _sl(T.h2, q)
    my_col = T.land[:, 8:9]

    sy.dma_start(x_own, T.x[:, :]).then_inc(S.xl, 16)
    pieces = []
    for j in order:
        if j // GT not in pieces:
            pieces.append(j // GT)
    for k, pc in enumerate(pieces):
        (act if k % 2 == 0 else sy).dma_start(T.at[:, GT * P * pc:GT * P * (pc + 1)],
                                              T.a[:, GT * P * pc:GT * P * (pc + 1)]).then_inc(S["al%d" % pc], 16)

    v.memset(T.ones[:, :], 1.0).then_inc(S.init, 1)
    v.memset(T.land[:, 8:12], 0.0).then_inc(S.init, 1)
    v.wait_ge(S.init, 2)
    pe.wait_ge(S.init, 2)
    g.wait_ge(S.init, 2)
    g.affine_select(T.idn[:, :], T.ones[:, 0:2 * B], [[-1, 2 * B]], Alu.is_equal, 0.0, 0, 1).then_inc(S.idn, 1)

    out = [pl["relay"][q]] + [cores[j] for j in pl["direct"][q]]
    left = 0
    g.wait_ge(S.xl, 16)
    left += _send(g, topo, core, out, x_own, [x_own for _ in out], S["xa%d" % q], S.sent)
    g.wait_ge(S.uc, 1)
    left += _send(g, topo, core, out, u_own, [u_own for _ in out], S["ua%d" % q], S.sent)
    to_hubs = [h for h in hubs if h != q]
    g.wait_ge(S.col, 1)
    left += _send(g, topo, core, [cores[h] for h in to_hubs], my_col,
                  [T.land[:, (q if q < h else q - 1):(q if q < h else q - 1) + 1] for h in to_hubs], S.cin, S.sent)
    if is_hub:
        n_in = sum(_bits(_mask(topo, cores[i], [cores[h] for h in hubs if h != i])) for i in range(N) if i != q)
        g.wait_ge(S.cin, n_in)
        mine = [cores[p] for p in pl["partners"][q]]
        left += _send(g, topo, core, mine, T.land[:, 0:N], [T.fin[:, 0:N] for _ in mine], S.cfin, S.sent)
    else:
        hub = [h for h in hubs if q in pl["partners"][h]][0]
        n_fin = _bits(_mask(topo, cores[hub], [cores[p] for p in pl["partners"][hub]]))
    g.wait_ge(S.sent, left)

    seen = []
    for p, j in enumerate(order):
        if j == q:
            pe.wait_ge(S.xl, 16)
        else:
            pe.wait_ge(S["xa%d" % j], cnt[j])
        if j // GT not in seen:
            seen.append(j // GT)
            pe.wait_ge(S["al%d" % (j // GT)], 16)
        mm = pe.matmul(T.ups[:, 0:B], T.at[:, P * j:P * (j + 1)], _sl(T.h1, j), p == 0, p == N - 1)
    mm.then_inc(S.u, 1)

    def s_mm(p):
        j = order[p]
        pe.wait_ge(S["sq%d" % j], 1)
        return pe.matmul(T.sps[:, 0:B], T.ones[:, :], _sl(T.sq, j), p == 0, p == N - 1)

    early = N - 1 - pl["late"][q]
    for p, j in enumerate(order):
        if j == q:
            pe.wait_ge(S.uc, 1)
        else:
            pe.wait_ge(S["ua%d" % j], cnt[j])
        mm = pe.matmul(T.wps[:, 0:B], T.at[:, P * j:P * (j + 1)], _sl(T.h2, j), p == 0, p == N - 1)
        if p == N - 1:
            mm.then_inc(S.w, 1)
        if 1 <= p <= early:
            s_mm(p - 1)
    pe.wait_ge(S.pa, 1)
    pe.wait_ge(S.pv, 1)
    pe.matmul(T.qps[0:2 * B, 0:1], T.prod[:, :], T.ones[:, 0:1], True, True).then_inc(S.pq, 1)
    for p in range(early, N):
        mm = s_mm(p)
    mm.then_inc(S.ssum, 1)
    pe.wait_ge(S.xq, 1)
    pe.matmul(T.fps[:, 0:B], T.ones[:, :], T.xq[:, :], True, False)
    pe.wait_ge(S.es, 1)
    pe.matmul(T.fps[:, 0:B], T.ones[:, :], T.es[:, :], False, True).then_inc(S.f, 1)

    for j in order:
        if j == q:
            act.wait_ge(S.uc, 1)
        else:
            act.wait_ge(S["ua%d" % j], cnt[j])
        act.activation(_sl(T.sq, j), _sl(T.h2, j), Act.Square).then_inc(S["sq%d" % j], 1)
    act.wait_ge(S.wc, 1)
    act.activation(T.prod[:, 0:B], T.wsb[:, :], Act.Square).then_inc(S.pa, 1)
    act.wait_ge(S.ssum, 1)
    act.activation(T.rr[:, :], T.sps[:, 0:B], Act.Sqrt).then_inc(S.r, 1)
    act.activation(T.r2[:, :], T.sps[:, 0:B], Act.Sqrt, scale=4.0).then_inc(S.r2, 1)
    act.activation(T.xq[:, :], T.sps[:, 0:B], Act.Square, scale=1.0 / math.sqrt(P)).then_inc(S.xq, 1)
    act.wait_ge(S.f, 1)
    act.activation(T.rt[:, :], T.fps[:, 0:B], Act.Sqrt).then_inc(S.rt, 1)

    v.wait_ge(S.u, 1)
    v.tensor_copy(u_own, T.ups[:, 0:B]).then_inc(S.uc, 1)
    v.wait_ge(S.w, 1)
    v.tensor_copy(T.wsb[:, :], T.wps[:, 0:B]).then_inc(S.wc, 1)
    v.wait_ge(S.wc, 1)
    v.wait_ge(S.uc, 1)
    v.tensor_tensor(T.prod[:, B:2 * B], T.wsb[:, :], u_own, Alu.mult).then_inc(S.pv, 1)
    v.wait_ge(S.pq, 1)
    v.tensor_copy(T.land[0:2 * B, 8:9], T.qps[0:2 * B, 0:1]).then_inc(S.col, 1)
    v.wait_ge(S.r, 1)
    v.tensor_tensor(T.t1[:, :], T.rr[:, :], u_own, Alu.mult).then_inc(S.t1, 1)
    v.wait_ge(S.t1, 1)
    v.tensor_tensor(T.vp[:, :], T.t1[:, :], T.wsb[:, :], Alu.add).then_inc(S.vp, 1)
    v.wait_ge(S.r2, 1)
    v.wait_ge(S.idn, 1)
    v.tensor_tensor(T.e1[:, :], T.r2[:, :], T.idn[:, B:2 * B], Alu.mult).then_inc(S.e1, 1)
    v.wait_ge(S.e1, 1)
    v.tensor_tensor(T.ee[:, :], T.e1[:, :], T.idn[:, 0:B], Alu.add).then_inc(S.ee, 1)
    v.wait_ge(S.ee, 1)
    v.wait_ge(S.vp, 1)
    v.wait_ge(S.xl, 16)
    if is_hub:
        v.wait_ge(S.col, 1)
        v.wait_ge(S.cin, n_in)
        cols = T.land[:, 0:N]
    else:
        v.wait_ge(S.cfin, n_fin)
        cols = T.fin[:, 0:N]
    v.tensor_reduce(T.s3[:, 0:1], cols, AxisListType.X, Alu.add).then_inc(S.s3, 1)
    v.wait_ge(S.s3, 1)
    v.tensor_scalar(T.es[:, :], T.ee[:, :], T.s3[:, 0:1], None, Alu.mult).then_inc(S.es, 1)
    v.wait_ge(S.rt, 1)
    v.reciprocal(T.rs[:, :], T.rt[:, :]).then_inc(S.rs, 1)
    v.wait_ge(S.rs, 1)
    v.tensor_tensor(T.y1[:, :], T.vp[:, :], T.rs[:, :], Alu.mult).then_inc(S.y1, 1)
    v.wait_ge(S.y1, 1)
    v.tensor_tensor(T.yo[:, :], T.y1[:, :], x_own, Alu.add).then_inc(S.y2, 1)

    sy.wait_ge(S.y2, 1)
    sy.dma_start(T.y[:, :], T.yo[:, :]).then_inc(S.st, 16)
    sy.wait_ge(S.st, 16)
